import numpy as np
import ml_dtypes


def mxq(x, axis, fmt="e4m3"):
    dtype, down = {"e4m3": (ml_dtypes.float8_e4m3fn, 7), "e5m2": (ml_dtypes.float8_e5m2, 14)}[fmt]
    v = np.moveaxis(np.asarray(x, np.float32).astype(ml_dtypes.bfloat16).astype(np.float64), axis, -1)
    blocks = v.reshape(v.shape[:-1] + (-1, 32))
    amax = np.abs(blocks).max(-1, keepdims=True)
    byte = np.maximum(np.where(amax > 0, np.frexp(amax)[1] - 1 + 127, 0) - down, 1)
    scale = np.exp2(byte - 127.0)
    codes = (blocks / scale).astype(np.float32).astype(dtype).astype(np.float64)
    return np.moveaxis((codes * scale).reshape(v.shape), -1, axis)


WIDE = False


def mx_kscale(k):
    if not WIDE:
        return np.ones(k)
    levels = np.array([10, -10, 5, -5, 0])
    if k % 512:
        return np.exp2(np.random.permutation(np.resize(levels, k // 32))).repeat(32)
    a = np.empty((k // 512, 16))
    for p in range(k // 512):
        a[p, :8] = np.random.permutation(np.resize(levels, 8))
        for g in range(8):
            far = levels[np.abs(levels - a[p, g]) >= 10]
            a[p, g + 8] = far[np.random.randint(len(far))]
    return np.exp2(a.ravel()).repeat(32)


def f64(x):
    return np.asarray(x).astype(np.float64)


def striped8(idx):
    return np.asarray(idx).reshape(8, -1, 16).transpose(0, 2, 1).reshape(128, -1).astype(np.uint16)


def unstriped8(offs):
    return offs.reshape(8, 16, -1).transpose(0, 2, 1).reshape(8, -1).astype(np.int64)


def pick8(x, idx, run):
    r = np.arange(len(x))
    return x[r[:, None], idx[r % (8 * run) // run]]


E2M1 = np.array([0.0, 0.5, 1.0, 1.5, 2.0, 3.0, 4.0, 6.0, -0.0, -0.5, -1.0, -1.5, -2.0, -3.0, -4.0, -6.0])


def pack_weight(w, fmt):
    k, n = w.shape
    w = f64(np.asarray(w, np.float32).astype(ml_dtypes.bfloat16)).reshape(k // 32, 32, n)
    amax = np.abs(w).max(1)
    if fmt == "e4m3":
        byte = np.frexp(amax)[1] - 1 + 127 - 7
    else:
        mant, ex = np.frexp(amax / 6.0)
        byte = np.where(mant > 0.5, ex, ex - 1) + 127
    byte = np.clip(np.where(amax > 0, byte, 1), 1, 254)
    scaled = (w * np.exp2(127.0 - byte)[:, None, :]).reshape(k, n).astype(np.float32)
    by_word = np.ascontiguousarray(scaled.reshape(k // 512, 128, 4, n).transpose(0, 1, 3, 2))
    if fmt == "e4m3":
        words = by_word.astype(ml_dtypes.float8_e4m3fn).view(np.uint8)
    else:
        c = by_word.astype(ml_dtypes.float4_e2m1fn).view(np.uint8) & 0xF
        words = (c[..., 0::2] | (c[..., 1::2] << 4)).reshape(k // 512, 128, 2 * n)
    return np.ascontiguousarray(words), np.ascontiguousarray(byte.astype(np.uint8).reshape(k // 512, 16, n))


def unpack_weight(words, scales, fmt):
    g, _, n = scales.shape
    words = np.ascontiguousarray(words).reshape(g, 128, n, -1)
    if fmt == "e4m3":
        vals = words.view(ml_dtypes.float8_e4m3fn).astype(np.float64)
    else:
        nib = np.empty((g, 128, n, 4), np.uint8)
        nib[..., 0::2] = words & 0xF
        nib[..., 1::2] = words >> 4
        vals = E2M1[nib]
    vals = vals * np.repeat(np.exp2(scales.astype(np.float64) - 127.0), 8, axis=1)[..., None]
    return vals.transpose(0, 1, 3, 2).reshape(g * 512, n)


def sigmoid(v):
    return 1.0 / (1.0 + np.exp(-v))


D, V, Q, I = 512, 2048, 128, 512


def setup_inputs():
    n = np.random.standard_normal
    idx = np.stack([np.random.permutation(V)[:I] for _ in range(8)])
    idx2 = np.stack([np.random.permutation(V)[:I] for _ in range(8)])
    fd = mx_kscale(D)
    vocp = pack_weight(n((D, V)) / fd[:, None], "e2m1")
    return {
        "hid": (n((D, Q)) * 1.0 / np.sqrt(D) * fd[:, None]).astype(np.float32),
        "voc_words": vocp[0],
        "voc_scales": vocp[1],
        "sw": (np.random.uniform(0.5, 2.0, (1, I))).astype(np.float32),
        "dhid": (n((D, Q)) * 1.0 / np.sqrt(D) * fd[:, None]).astype(np.float32),
        "base": (0.5 * n((Q, V))).astype(np.float32),
        "offs": striped8(idx),
        "offs2": striped8(idx2),
    }


def reference(hid, voc_words, voc_scales, sw, dhid, base, offs, offs2):
    idx = unstriped8(offs)
    idx2 = unstriped8(offs2)
    vocu = unpack_weight(voc_words, voc_scales, "e2m1")
    hidq = mxq(f64(hid), 0, "e4m3")
    a = hidq.T @ vocu
    dhidq = mxq(f64(dhid), 0, "e4m3")
    ta = dhidq.T @ vocu
    m1 = np.max(a, axis=1, keepdims=True)
    p = np.exp(a - m1)
    z = np.sum(p, axis=1, keepdims=True)
    px = np.exp(pick8(a, idx, 16) - m1)
    px2 = np.exp(pick8(a, idx2, 16) - m1)
    u1 = sigmoid((px2 - px) / z * 512.0)
    dpx2 = f64(sw) * u1 * (1.0 - u1) * 512.0 / z
    dpx = f64(sw) * u1 * (1.0 - u1) * 512.0 / z * (-1.0)
    dz = np.sum(f64(sw) * u1 * (1.0 - u1) * 512.0 * (px2 - px) / np.square(z) * (-1.0), axis=1, keepdims=True)
    xp = ta * p
    xz = np.sum(xp, axis=1, keepdims=True)
    xpx = pick8(ta, idx, 16) * px
    xpx2 = pick8(ta, idx2, 16) * px2
    xu1 = (xpx2 - xpx - xz * (px2 - px) / z) / z * 512.0 * u1 * (1.0 - u1)
    xdpx2 = ((xu1 * f64(sw) * (1.0 - u1) + xu1 * (-1.0) * f64(sw) * u1) * 512.0 - xz * f64(sw) * u1 * (1.0 - u1) * 512.0 / z) / z
    xdpx = ((xu1 * f64(sw) * (1.0 - u1) + xu1 * (-1.0) * f64(sw) * u1) * 512.0 - xz * f64(sw) * u1 * (1.0 - u1) * 512.0 / z) / z * (-1.0)
    xdz = np.sum(((xu1 * f64(sw) * (1.0 - u1) + xu1 * (-1.0) * f64(sw) * u1) * 512.0 * (px2 - px) + (xpx2 - xpx) * f64(sw) * u1 * (1.0 - u1) * 512.0 - xz * z * 2.0 * f64(sw) * u1 * (1.0 - u1) * 512.0 * (px2 - px) / np.square(z)) / np.square(z) * (-1.0), axis=1, keepdims=True)
    xe1 = xdpx2 * px2 + xpx2 * dpx2
    xs1 = np.zeros((Q, V))
    xs1[np.arange(Q)[:, None], idx2[np.arange(Q) % 128 // 16]] = xe1
    xe2 = xdpx * px + xpx * dpx
    xs2 = np.zeros((Q, V))
    xs2[np.arange(Q)[:, None], idx[np.arange(Q) % 128 // 16]] = xe2
    xda = xdz * p + xp * dz + xs1 + xs2
    y = xda * 2.0 + f64(base)
    return y

@@ -1,0 +1,232 @@
+from contextlib import ExitStack
+
+import concourse.mybir as mybir
+from concourse.masks import make_identity
+
+D, V, Q, I = 512, 2048, 128, 512
+FLOPS = 2 * 2 * D * V * Q
+
+F32 = mybir.dt.float32
+BF16 = mybir.dt.bfloat16
+I32 = mybir.dt.int32
+U32 = mybir.dt.uint32
+U16 = mybir.dt.uint16
+U8 = mybir.dt.uint8
+FP8X4 = mybir.dt.float8_e4m3fn_x4
+FP4X4 = mybir.dt.float4_e2m1fn_x4
+ALU = mybir.AluOpType
+ACT = mybir.ActivationFunctionType
+AX = mybir.AxisListType
+
+P = 128
+PACK = 4
+NB = 512
+BANKS = V // NB
+BLK = NB // P
+SHARP = 512.0
+
+
+def tile_attend_hvrankshares_heads_kernel(tc, hid, voc_words, voc_scales, sw, dhid, base, offs, offs2, out):
+    nc = tc.nc
+    with ExitStack() as ctx:
+        keep = ctx.enter_context(tc.tile_pool(name="keep", bufs=1))
+        psum = ctx.enter_context(tc.psum_pool(name="psum", bufs=1))
+
+        def cols(j):
+            return slice(j * NB, (j + 1) * NB)
+
+        def one(j):
+            return slice(j, j + 1)
+
+        list1 = keep.tile([P, I // 16], U16, name="list1")
+        list2 = keep.tile([P, I // 16], U16, name="list2")
+        vscale = keep.tile([P, V], U8, name="vscale", align_bytes=64)
+        nc.vector.memset(vscale[:].bitcast(I32), 0)
+
+        hid_raw = keep.tile([P, PACK, Q], F32, name="hid_raw", tag="stage_h")
+        nc.sync.dma_start(out=hid_raw[:], in_=hid.rearrange("(p j) q -> p j q", j=PACK))
+        scale_rows = voc_scales[0].bitcast(I32).rearrange("(g r) c -> r g c", r=4)
+        for r in range(4):
+            nc.sync.dma_start(out=vscale[r:P:32, :].bitcast(I32), in_=scale_rows[r])
+        words = []
+        for h in range(2):
+            half = keep.tile([P, V], U8, name="words%d" % h, align_bytes=64)
+            nc.sync.dma_start(out=half[:].bitcast(I32), in_=voc_words[0][:, h * V:(h + 1) * V].bitcast(I32))
+            words.append(half)
+        dhid_raw = keep.tile([P, PACK, Q], F32, name="dhid_raw", tag="stage_d")
+        nc.sync.dma_start(out=dhid_raw[:], in_=dhid.rearrange("(p j) q -> p j q", j=PACK))
+        nc.sync.dma_start(list2[:], offs2)
+        nc.sync.dma_start(list1[:], offs)
+
+        factors = keep.tile([P, 4], F32, name="factors")
+        for j, value in enumerate((SHARP / 2, -SHARP / 2, -SHARP, -1.0)):
+            nc.vector.memset(factors[:, one(j)], value)
+        warm = keep.tile([P, 1], F32, name="warm")
+        nc.scalar.activation(out=warm[:], in_=factors[:, one(3)], func=ACT.Exp)
+
+        win2 = keep.tile([P, V], F32, name="win2")
+        win1 = keep.tile([P, V], F32, name="win1")
+        nc.vector.memset(win2[:], 0.0)
+        ident = keep.tile([P, P], F32, name="ident")
+        make_identity(nc, ident[:])
+        nc.gpsimd.memset(win1[:], 0.0)
+
+        hid_bf = keep.tile([P, Q, PACK], BF16, name="hid_bf", align_bytes=64)
+        dhid_bf = keep.tile([P, Q, PACK], BF16, name="dhid_bf", align_bytes=64)
+        hq = keep.tile([P, Q], U32, name="hq", align_bytes=64)
+        hs = keep.tile([P, Q], U8, name="hs", align_bytes=64)
+        dq = keep.tile([P, Q], U32, name="dq", align_bytes=64)
+        ds = keep.tile([P, Q], U8, name="ds", align_bytes=64)
+        nc.vector.tensor_copy(out=hid_bf[:], in_=hid_raw[:].rearrange("p j q -> p q j"))
+        nc.vector.quantize_mx(out=hq[:].bitcast(FP8X4), scales=hs[:], in_=hid_bf[:].rearrange("p q j -> p (q j)"))
+        nc.scalar.copy(out=dhid_bf[:], in_=dhid_raw[:].rearrange("p j q -> p q j"))
+        nc.vector.quantize_mx(out=dq[:].bitcast(FP8X4), scales=ds[:], in_=dhid_bf[:].rearrange("p q j -> p (q j)"))
+
+        sw_all = keep.tile([P, I], F32, name="sw_all", tag="stage_d")
+        nc.sync.dma_start(out=sw_all[:], in_=sw[0].partition_broadcast(P))
+        base_sb = keep.tile([P, V], F32, name="base_sb", tag="stage_h")
+        nc.sync.dma_start(out=base_sb[:], in_=base)
+
+        bank_a = [psum.tile([P, NB], F32, name="bank_a%d" % j) for j in range(BANKS)]
+        bank_t = [psum.tile([P, NB], F32, name="bank_t%d" % j) for j in range(BANKS)]
+
+        def product(bank, codes, scales, j):
+            lo = (j % 2) * 2 * NB
+            nc.tensor.matmul_mx(out=bank[:], lhsT=codes[:].bitcast(FP8X4), lhsT_scale=scales[:],
+                                rhs=words[j // 2][:, lo:lo + 2 * NB].bitcast(FP4X4), rhs_scale=vscale[:, cols(j)],
+                                start=True, stop=True)
+
+        for j in range(BANKS):
+            product(bank_a[j], hq, hs, j)
+        for j in range(BANKS):
+            product(bank_t[j], dq, ds, j)
+
+        a_sb = keep.tile([P, V], F32, name="a_sb")
+        ta_sb = keep.tile([P, V], F32, name="ta_sb")
+        p_sb = keep.tile([P, V], F32, name="p_sb")
+        xp_sb = keep.tile([P, V], F32, name="xp_sb")
+        mx = keep.tile([P, BANKS], F32, name="mx")
+        neg_mx = keep.tile([P, BANKS], F32, name="neg_mx")
+        zpart = keep.tile([P, BANKS], F32, name="zpart")
+        xzpart = keep.tile([P, BANKS], F32, name="xzpart")
+        for j in range(BANKS):
+            nc.vector.tensor_scalar(out=a_sb[:, cols(j)], in0=bank_a[j][:], scalar1=1.0, scalar2=None,
+                                    op0=ALU.mult, op1=ALU.max, accum_out=mx[:, one(j)])
+            nc.gpsimd.tensor_scalar(out=neg_mx[:, one(j)], in0=mx[:, one(j)], scalar1=-1.0, scalar2=0.0,
+                                    op0=ALU.mult, op1=ALU.add)
+            nc.scalar.activation(out=p_sb[:, cols(j)], in_=a_sb[:, cols(j)], func=ACT.Exp,
+                                 bias=neg_mx[:, one(j)], accum_out=zpart[:, one(j)])
+        neg_m = keep.tile([P, 1], F32, name="neg_m")
+        nc.vector.tensor_reduce(out=neg_m[:], in_=mx[:], axis=AX.X, op=ALU.max, negate=True)
+        shift = keep.tile([P, BANKS], F32, name="shift")
+        nc.scalar.activation(out=shift[:], in_=mx[:], func=ACT.Exp, bias=neg_m[:])
+
+        def vec(name):
+            return keep.tile([P, I], F32, name=name)
+
+        ga2, ga1, px, px2 = vec("ga2"), vec("ga1"), vec("px"), vec("px2")
+        nc.vector.tensor_copy(ga2[:], a_sb[:].indirect(list2[:]))
+        nc.vector.tensor_copy(ga1[:], a_sb[:].indirect(list1[:]))
+        nc.scalar.copy(out=ta_sb[:, cols(0)], in_=bank_t[0][:])
+        nc.scalar.activation(out=px2[:], in_=ga2[:], func=ACT.Exp, bias=neg_m[:])
+        nc.scalar.copy(out=ta_sb[:, cols(1)], in_=bank_t[1][:])
+        nc.scalar.activation(out=px[:], in_=ga1[:], func=ACT.Exp, bias=neg_m[:])
+        for j in range(2, BANKS):
+            nc.scalar.copy(out=ta_sb[:, cols(j)], in_=bank_t[j][:])
+
+        zs = keep.tile([P, BANKS], F32, name="zs")
+        z = keep.tile([P, 1], F32, name="z")
+        rz = keep.tile([P, 1], F32, name="rz")
+        rf = keep.tile([P, 4], F32, name="rf")
+        neg_share = keep.tile([P, BANKS], F32, name="neg_share")
+        xzs = keep.tile([P, BANKS], F32, name="xzs")
+        neg_e = keep.tile([P, 1], F32, name="neg_e")
+        delta, th, sq = vec("delta"), vec("th"), vec("sq")
+
+        def xp_bank(j):
+            nc.vector.scalar_tensor_tensor(out=xp_sb[:, cols(j)], in0=bank_t[j][:], scalar=shift[:, one(j)],
+                                           in1=p_sb[:, cols(j)], op0=ALU.mult, op1=ALU.mult,
+                                           accum_out=xzpart[:, one(j)])
+
+        nc.vector.scalar_tensor_tensor(out=zs[:], in0=zpart[:], scalar=1.0, in1=shift[:], op0=ALU.mult, op1=ALU.mult,
+                                       accum_out=z[:])
+        xp_bank(0)
+        nc.vector.reciprocal(rz[:], z[:])
+        xp_bank(1)
+        nc.vector.tensor_scalar(out=rf[:], in0=factors[:], scalar1=rz[:], scalar2=None, op0=ALU.mult)
+        xp_bank(2)
+        nc.vector.tensor_tensor(out=delta[:], in0=px2[:], in1=px[:], op=ALU.subtract)
+        xp_bank(3)
+        nc.scalar.activation(out=th[:], in_=delta[:], func=ACT.Tanh, scale=rf[:, one(0)])
+        nc.scalar.activation(out=sq[:], in_=th[:], func=ACT.Square)
+        nc.scalar.activation(out=neg_share[:], in_=shift[:], func=ACT.Copy, scale=rf[:, one(3)])
+
+        t2, t1 = vec("t2"), vec("t1")
+        nc.vector.tensor_copy(t2[:], ta_sb[:].indirect(list2[:]))
+        nc.vector.tensor_scalar(out=xzs[:], in0=xzpart[:], scalar1=rf[:, one(3)], scalar2=None, op0=ALU.mult,
+                                op1=ALU.add, accum_out=neg_e[:])
+
+        def stt(name, in0, scalar, in1, op0, op1, accum=None):
+            res = vec(name)
+            nc.vector.scalar_tensor_tensor(out=res[:], in0=in0[:], scalar=scalar, in1=in1[:], op0=op0, op1=op1,
+                                           accum_out=accum)
+            return res
+
+        def tt(name, in0, in1, op):
+            res = vec(name)
+            nc.vector.tensor_tensor(out=res[:], in0=in0[:], in1=in1[:], op=op)
+            return res
+
+        gsum = keep.tile([P, 2], F32, name="gsum")
+        ssum = keep.tile([P, 5], F32, name="ssum")
+        gn = stt("gn", sq, -1.0, sw_all, ALU.add, ALU.mult)
+        nc.vector.tensor_copy(t1[:], ta_sb[:].indirect(list1[:]))
+        gs2 = stt("gs2", gn, rf[:, one(1)], px2, ALU.mult, ALU.mult, gsum[:, one(0)])
+        gs1 = stt("gs1", gn, rf[:, one(0)], px, ALU.mult, ALU.mult, gsum[:, one(1)])
+        y2 = stt("y2", t2, neg_e[:], gs2, ALU.add, ALU.mult, ssum[:, one(0)])
+        y1 = stt("y1", t1, neg_e[:], gs1, ALU.add, ALU.mult, ssum[:, one(1)])
+        ysum = tt("ysum", y2, y1, ALU.add)
+        bend = stt("bend", ysum, rf[:, one(2)], th, ALU.mult, ALU.mult)
+        b2 = stt("b2", bend, 1.0, px2, ALU.mult, ALU.mult, ssum[:, one(2)])
+        b1 = stt("b1", bend, -1.0, px, ALU.mult, ALU.mult, ssum[:, one(3)])
+        nc.vector.tensor_tensor(win2[:].indirect(list2[:]), y2[:], b2[:], ALU.add)
+        nc.vector.tensor_tensor(win1[:].indirect(list1[:]), y1[:], b1[:], ALU.add)
+
+        def turn_add(src, first, last):
+            for j in range(BANKS):
+                for b in range(BLK):
+                    c0 = j * NB + b * P
+                    nc.tensor.matmul(out=bank_a[j][:, b * P:(b + 1) * P], lhsT=src[:, c0:c0 + P], rhs=ident[:],
+                                     start=(first and b == 0), stop=(last and b == BLK - 1), is_transpose=True)
+
+        turn_add(base_sb, True, False)
+
+        scrap2 = keep.tile([P, 2], F32, name="scrap2")
+        scrap2b = keep.tile([P, 2], F32, name="scrap2b")
+        scrap3 = keep.tile([P, 5], F32, name="scrap3")
+        beta = keep.tile([P, 1], F32, name="beta")
+        stot = keep.tile([P, 1], F32, name="stot")
+        alpha = keep.tile([P, BANKS], F32, name="alpha")
+        nc.scalar.activation(out=scrap2[:], in_=gsum[:], func=ACT.Copy, scale=rf[:, one(3)], accum_out=beta[:])
+        nc.scalar.activation(out=scrap2b[:], in_=gsum[:], func=ACT.Copy, scale=neg_e[:], accum_out=ssum[:, one(4)])
+        bxp = keep.tile([P, V], F32, name="bxp")
+        for j in range(BANKS):
+            nc.scalar.activation(out=bxp[:, cols(j)], in_=xp_sb[:, cols(j)], func=ACT.Copy, scale=beta[:])
+        turn_add(bxp, False, False)
+        nc.scalar.activation(out=scrap3[:], in_=ssum[:], func=ACT.Copy, accum_out=stot[:])
+        nc.scalar.activation(out=alpha[:], in_=neg_share[:], func=ACT.Copy, scale=stot[:])
+        ap = keep.tile([P, V], F32, name="ap")
+        for j in range(BANKS):
+            nc.scalar.activation(out=ap[:, cols(j)], in_=p_sb[:, cols(j)], func=ACT.Copy, scale=alpha[:, one(j)])
+        turn_add(ap, False, False)
+        turn_add(win2, False, True)
+
+        turned = keep.tile([P, V], F32, name="turned")
+        res = keep.tile([P, V], F32, name="res")
+        for j in range(BANKS):
+            nc.scalar.copy(out=turned[:, cols(j)], in_=bank_a[j][:])
+            for b in range(BLK):
+                c0 = j * NB + b * P
+                nc.tensor.transpose(bank_t[j][:, b * P:(b + 1) * P], turned[:, c0:c0 + P], ident[:])
+            nc.vector.tensor_tensor(out=res[:, cols(j)], in0=bank_t[j][:], in1=win1[:, cols(j)], op=ALU.add)
+            nc.sync.dma_start(out=out[:, cols(j)], in_=res[:, cols(j)])

@@ -64,12 +64,8 @@ def tile_attend_hvrankshares_heads_kernel(tc, hid, voc_words, voc_scales, sw, dh
         warm = keep.tile([P, 1], F32, name="warm")
         nc.scalar.activation(out=warm[:], in_=factors[:, one(3)], func=ACT.Exp)
 
-        win2 = keep.tile([P, V], F32, name="win2")
-        win1 = keep.tile([P, V], F32, name="win1")
-        nc.vector.memset(win2[:], 0.0)
         ident = keep.tile([P, P], F32, name="ident")
         make_identity(nc, ident[:])
-        nc.gpsimd.memset(win1[:], 0.0)
 
         hid_bf = keep.tile([P, Q, PACK], BF16, name="hid_bf", align_bytes=64)
         dhid_bf = keep.tile([P, Q, PACK], BF16, name="dhid_bf", align_bytes=64)
@@ -102,7 +98,7 @@ def tile_attend_hvrankshares_heads_kernel(tc, hid, voc_words, voc_scales, sw, dh
             product(bank_t[j], dq, ds, j)
 
         a_sb = keep.tile([P, V], F32, name="a_sb")
-        ta_sb = keep.tile([P, V], F32, name="ta_sb")
+        ta_sb = keep.tile([P, V], F32, name="ta_sb", tag="slot_ta")
         p_sb = keep.tile([P, V], F32, name="p_sb")
         xp_sb = keep.tile([P, V], F32, name="xp_sb")
         mx = keep.tile([P, BANKS], F32, name="mx")
@@ -121,17 +117,16 @@ def tile_attend_hvrankshares_heads_kernel(tc, hid, voc_words, voc_scales, sw, dh
         shift = keep.tile([P, BANKS], F32, name="shift")
         nc.scalar.activation(out=shift[:], in_=mx[:], func=ACT.Exp, bias=neg_m[:])
 
-        def vec(name):
-            return keep.tile([P, I], F32, name=name)
+        def vec(name, tag=None):
+            return keep.tile([P, I], F32, name=name, tag=tag or name)
 
         ga2, ga1, px, px2 = vec("ga2"), vec("ga1"), vec("px"), vec("px2")
         nc.vector.tensor_copy(ga2[:], a_sb[:].indirect(list2[:]))
         nc.vector.tensor_copy(ga1[:], a_sb[:].indirect(list1[:]))
-        nc.scalar.copy(out=ta_sb[:, cols(0)], in_=bank_t[0][:])
         nc.scalar.activation(out=px2[:], in_=ga2[:], func=ACT.Exp, bias=neg_m[:])
-        nc.scalar.copy(out=ta_sb[:, cols(1)], in_=bank_t[1][:])
+        nc.scalar.copy(out=ta_sb[:, cols(0)], in_=bank_t[0][:])
         nc.scalar.activation(out=px[:], in_=ga1[:], func=ACT.Exp, bias=neg_m[:])
-        for j in range(2, BANKS):
+        for j in range(1, BANKS):
             nc.scalar.copy(out=ta_sb[:, cols(j)], in_=bank_t[j][:])
 
         zs = keep.tile([P, BANKS], F32, name="zs")
@@ -153,9 +148,9 @@ def tile_attend_hvrankshares_heads_kernel(tc, hid, voc_words, voc_scales, sw, dh
         xp_bank(0)
         nc.vector.reciprocal(rz[:], z[:])
         xp_bank(1)
-        nc.vector.tensor_scalar(out=rf[:], in0=factors[:], scalar1=rz[:], scalar2=None, op0=ALU.mult)
+        nc.scalar.activation(out=rf[:], in_=factors[:], func=ACT.Copy, scale=rz[:])
         xp_bank(2)
-        nc.vector.tensor_tensor(out=delta[:], in0=px2[:], in1=px[:], op=ALU.subtract)
+        nc.gpsimd.tensor_tensor(out=delta[:], in0=px2[:], in1=px[:], op=ALU.subtract)
         xp_bank(3)
         nc.scalar.activation(out=th[:], in_=delta[:], func=ACT.Tanh, scale=rf[:, one(0)])
         nc.scalar.activation(out=sq[:], in_=th[:], func=ACT.Square)
@@ -163,63 +158,69 @@ def tile_attend_hvrankshares_heads_kernel(tc, hid, voc_words, voc_scales, sw, dh
 
         t2, t1 = vec("t2"), vec("t1")
         nc.vector.tensor_copy(t2[:], ta_sb[:].indirect(list2[:]))
-        nc.vector.tensor_scalar(out=xzs[:], in0=xzpart[:], scalar1=rf[:, one(3)], scalar2=None, op0=ALU.mult,
-                                op1=ALU.add, accum_out=neg_e[:])
+        nc.scalar.activation(out=xzs[:], in_=xzpart[:], func=ACT.Copy, scale=rf[:, one(3)], accum_out=neg_e[:])
 
-        def stt(name, in0, scalar, in1, op0, op1, accum=None):
-            res = vec(name)
-            nc.vector.scalar_tensor_tensor(out=res[:], in0=in0[:], scalar=scalar, in1=in1[:], op0=op0, op1=op1,
-                                           accum_out=accum)
-            return res
+        def stt(res, in0, scalar, in1, op0, op1, accum=None, part=slice(0, I)):
+            nc.vector.scalar_tensor_tensor(out=res[:, part], in0=in0[:, part], scalar=scalar, in1=in1[:, part],
+                                           op0=op0, op1=op1, accum_out=accum)
 
-        def tt(name, in0, in1, op):
-            res = vec(name)
-            nc.vector.tensor_tensor(out=res[:], in0=in0[:], in1=in1[:], op=op)
-            return res
-
+        halves = (slice(0, I // 2), slice(I // 2, I))
         gsum = keep.tile([P, 2], F32, name="gsum")
-        ssum = keep.tile([P, 5], F32, name="ssum")
-        gn = stt("gn", sq, -1.0, sw_all, ALU.add, ALU.mult)
+        ssum = keep.tile([P, 7], F32, name="ssum")
+        gn, gs2, gs1, y2, y1 = vec("gn", "slot_gn"), vec("gs2"), vec("gs1"), vec("y2"), vec("y1")
+        ysum, bend, b2, b1 = vec("ysum"), vec("bend"), vec("b2"), vec("b1")
         nc.vector.tensor_copy(t1[:], ta_sb[:].indirect(list1[:]))
-        gs2 = stt("gs2", gn, rf[:, one(1)], px2, ALU.mult, ALU.mult, gsum[:, one(0)])
-        gs1 = stt("gs1", gn, rf[:, one(0)], px, ALU.mult, ALU.mult, gsum[:, one(1)])
-        y2 = stt("y2", t2, neg_e[:], gs2, ALU.add, ALU.mult, ssum[:, one(0)])
-        y1 = stt("y1", t1, neg_e[:], gs1, ALU.add, ALU.mult, ssum[:, one(1)])
-        ysum = tt("ysum", y2, y1, ALU.add)
-        bend = stt("bend", ysum, rf[:, one(2)], th, ALU.mult, ALU.mult)
-        b2 = stt("b2", bend, 1.0, px2, ALU.mult, ALU.mult, ssum[:, one(2)])
-        b1 = stt("b1", bend, -1.0, px, ALU.mult, ALU.mult, ssum[:, one(3)])
+        stt(gn, sq, -1.0, sw_all, ALU.add, ALU.mult)
+        stt(gs2, gn, rf[:, one(1)], px2, ALU.mult, ALU.mult, gsum[:, one(0)])
+        stt(gs1, gn, rf[:, one(0)], px, ALU.mult, ALU.mult, gsum[:, one(1)])
+        win2 = keep.tile([P, V], F32, name="win2", tag="slot_ta")
+        nc.gpsimd.memset(win2[:], 0.0)
+        win1 = keep.tile([P, V], F32, name="win1", tag="slot_gn")
+        nc.gpsimd.memset(win1[:], 0.0)
+        stt(y2, t2, neg_e[:], gs2, ALU.add, ALU.mult, ssum[:, one(0)])
+        for h, part in enumerate(halves):
+            stt(y1, t1, neg_e[:], gs1, ALU.add, ALU.mult, ssum[:, one(1 + h)], part)
+        for part in halves:
+            nc.vector.tensor_tensor(out=ysum[:, part], in0=y2[:, part], in1=y1[:, part], op=ALU.add)
+        for part in halves:
+            stt(bend, ysum, rf[:, one(2)], th, ALU.mult, ALU.mult, None, part)
+        for h, part in enumerate(halves):
+            stt(b2, bend, 1.0, px2, ALU.mult, ALU.mult, ssum[:, one(3 + h)], part)
+        stt(b1, bend, -1.0, px, ALU.mult, ALU.mult, ssum[:, one(5)])
         nc.vector.tensor_tensor(win2[:].indirect(list2[:]), y2[:], b2[:], ALU.add)
         nc.vector.tensor_tensor(win1[:].indirect(list1[:]), y1[:], b1[:], ALU.add)
 
-        def turn_add(src, first, last):
-            for j in range(BANKS):
-                for b in range(BLK):
-                    c0 = j * NB + b * P
-                    nc.tensor.matmul(out=bank_a[j][:, b * P:(b + 1) * P], lhsT=src[:, c0:c0 + P], rhs=ident[:],
-                                     start=(first and b == 0), stop=(last and b == BLK - 1), is_transpose=True)
+        def turn_add(src, j, blocks, first=False, last=False):
+            for b in blocks:
+                c0 = j * NB + b * P
+                nc.tensor.matmul(out=bank_a[j][:, b * P:(b + 1) * P], lhsT=src[:, c0:c0 + P], rhs=ident[:],
+                                 start=(first and b == 0), stop=(last and b == BLK - 1), is_transpose=True)
 
-        turn_add(base_sb, True, False)
+        for j in range(BANKS):
+            turn_add(base_sb, j, range(BLK), first=True)
 
         scrap2 = keep.tile([P, 2], F32, name="scrap2")
         scrap2b = keep.tile([P, 2], F32, name="scrap2b")
-        scrap3 = keep.tile([P, 5], F32, name="scrap3")
+        scrap3 = keep.tile([P, 7], F32, name="scrap3")
         beta = keep.tile([P, 1], F32, name="beta")
         stot = keep.tile([P, 1], F32, name="stot")
         alpha = keep.tile([P, BANKS], F32, name="alpha")
         nc.scalar.activation(out=scrap2[:], in_=gsum[:], func=ACT.Copy, scale=rf[:, one(3)], accum_out=beta[:])
-        nc.scalar.activation(out=scrap2b[:], in_=gsum[:], func=ACT.Copy, scale=neg_e[:], accum_out=ssum[:, one(4)])
+        nc.scalar.activation(out=scrap2b[:], in_=gsum[:], func=ACT.Copy, scale=neg_e[:], accum_out=ssum[:, one(6)])
         bxp = keep.tile([P, V], F32, name="bxp")
         for j in range(BANKS):
             nc.scalar.activation(out=bxp[:, cols(j)], in_=xp_sb[:, cols(j)], func=ACT.Copy, scale=beta[:])
-        turn_add(bxp, False, False)
+            turn_add(bxp, j, range(BLK))
         nc.scalar.activation(out=scrap3[:], in_=ssum[:], func=ACT.Copy, accum_out=stot[:])
         nc.scalar.activation(out=alpha[:], in_=neg_share[:], func=ACT.Copy, scale=stot[:])
         ap = keep.tile([P, V], F32, name="ap")
+        for blocks in (range(0, BLK - 1), range(BLK - 1, BLK)):
+            for j in range(BANKS):
+                span = slice(j * NB + blocks.start * P, j * NB + blocks.stop * P)
+                nc.scalar.activation(out=ap[:, span], in_=p_sb[:, span], func=ACT.Copy, scale=alpha[:, one(j)])
+                turn_add(ap, j, blocks)
         for j in range(BANKS):
-            nc.scalar.activation(out=ap[:, cols(j)], in_=p_sb[:, cols(j)], func=ACT.Copy, scale=alpha[:, one(j)])
-        turn_add(ap, False, False)
-        turn_add(win2, False, True)
+            turn_add(win2, j, range(BLK), last=True)
 
         turned = keep.tile([P, V], F32, name="turned")
         res = keep.tile([P, V], F32, name="res")
@@ -228,5 +229,9 @@ def tile_attend_hvrankshares_heads_kernel(tc, hid, voc_words, voc_scales, sw, dh
             for b in range(BLK):
                 c0 = j * NB + b * P
                 nc.tensor.transpose(bank_t[j][:, b * P:(b + 1) * P], turned[:, c0:c0 + P], ident[:])
-            nc.vector.tensor_tensor(out=res[:, cols(j)], in0=bank_t[j][:], in1=win1[:, cols(j)], op=ALU.add)
-            nc.sync.dma_start(out=out[:, cols(j)], in_=res[:, cols(j)])
+        pieces = [(0, 0, NB), (1, 0, NB), (2, 0, NB), (3, 0, NB // 2), (3, NB // 2, NB)]
+        for n, (j, lo, hi) in enumerate(pieces):
+            span = slice(j * NB + lo, j * NB + hi)
+            nc.vector.tensor_tensor(out=res[:, span], in0=bank_t[j][:, lo:hi], in1=win1[:, span], op=ALU.add)
+            queue = nc.sync if n % 2 == 0 else nc.scalar
+            queue.dma_start(out=out[:, span], in_=res[:, span])

@@ -48,13 +48,11 @@ def tile_attend_hvrankshares_heads_kernel(tc, hid, voc_words, voc_scales, sw, dh
         scale_rows = voc_scales[0].bitcast(I32).rearrange("(g r) c -> r g c", r=4)
         for r in range(4):
             nc.sync.dma_start(out=vscale[r:P:32, :].bitcast(I32), in_=scale_rows[r])
-        words = []
-        for h in range(2):
-            half = keep.tile([P, V], U8, name="words%d" % h, align_bytes=64)
-            nc.sync.dma_start(out=half[:].bitcast(I32), in_=voc_words[0][:, h * V:(h + 1) * V].bitcast(I32))
-            words.append(half)
+        words = [keep.tile([P, V], U8, name="words%d" % h, align_bytes=64) for h in range(2)]
         dhid_raw = keep.tile([P, PACK, Q], F32, name="dhid_raw", tag="stage_d")
+        nc.sync.dma_start(out=words[0][:].bitcast(I32), in_=voc_words[0][:, 0:V].bitcast(I32))
         nc.sync.dma_start(out=dhid_raw[:], in_=dhid.rearrange("(p j) q -> p j q", j=PACK))
+        nc.sync.dma_start(out=words[1][:].bitcast(I32), in_=voc_words[0][:, V:2 * V].bitcast(I32))
         nc.sync.dma_start(list2[:], offs2)
         nc.sync.dma_start(list1[:], offs)
 
@@ -123,11 +121,10 @@ def tile_attend_hvrankshares_heads_kernel(tc, hid, voc_words, voc_scales, sw, dh
         ga2, ga1, px, px2 = vec("ga2"), vec("ga1"), vec("px"), vec("px2")
         nc.vector.tensor_copy(ga2[:], a_sb[:].indirect(list2[:]))
         nc.vector.tensor_copy(ga1[:], a_sb[:].indirect(list1[:]))
-        nc.scalar.activation(out=px2[:], in_=ga2[:], func=ACT.Exp, bias=neg_m[:])
         nc.scalar.copy(out=ta_sb[:, cols(0)], in_=bank_t[0][:])
+        nc.scalar.activation(out=px2[:], in_=ga2[:], func=ACT.Exp, bias=neg_m[:])
+        nc.scalar.copy(out=ta_sb[:, cols(1)], in_=bank_t[1][:])
         nc.scalar.activation(out=px[:], in_=ga1[:], func=ACT.Exp, bias=neg_m[:])
-        for j in range(1, BANKS):
-            nc.scalar.copy(out=ta_sb[:, cols(j)], in_=bank_t[j][:])
 
         zs = keep.tile([P, BANKS], F32, name="zs")
         z = keep.tile([P, 1], F32, name="z")
@@ -145,13 +142,15 @@ def tile_attend_hvrankshares_heads_kernel(tc, hid, voc_words, voc_scales, sw, dh
 
         nc.vector.scalar_tensor_tensor(out=zs[:], in0=zpart[:], scalar=1.0, in1=shift[:], op0=ALU.mult, op1=ALU.mult,
                                        accum_out=z[:])
-        xp_bank(0)
-        nc.vector.reciprocal(rz[:], z[:])
-        xp_bank(1)
-        nc.scalar.activation(out=rf[:], in_=factors[:], func=ACT.Copy, scale=rz[:])
-        xp_bank(2)
-        nc.gpsimd.tensor_tensor(out=delta[:], in0=px2[:], in1=px[:], op=ALU.subtract)
         xp_bank(3)
+        nc.scalar.copy(out=ta_sb[:, cols(3)], in_=bank_t[3][:])
+        nc.vector.reciprocal(rz[:], z[:])
+        xp_bank(2)
+        nc.scalar.copy(out=ta_sb[:, cols(2)], in_=bank_t[2][:])
+        nc.scalar.activation(out=rf[:], in_=factors[:], func=ACT.Copy, scale=rz[:])
+        xp_bank(1)
+        nc.gpsimd.tensor_tensor(out=delta[:], in0=px2[:], in1=px[:], op=ALU.subtract)
+        xp_bank(0)
         nc.scalar.activation(out=th[:], in_=delta[:], func=ACT.Tanh, scale=rf[:, one(0)])
         nc.scalar.activation(out=sq[:], in_=th[:], func=ACT.Square)
         nc.scalar.activation(out=neg_share[:], in_=shift[:], func=ACT.Copy, scale=rf[:, one(3)])
@@ -218,13 +217,17 @@ def tile_attend_hvrankshares_heads_kernel(tc, hid, voc_words, voc_scales, sw, dh
             for j in range(BANKS):
                 span = slice(j * NB + blocks.start * P, j * NB + blocks.stop * P)
                 nc.scalar.activation(out=ap[:, span], in_=p_sb[:, span], func=ACT.Copy, scale=alpha[:, one(j)])
-                turn_add(ap, j, blocks)
-        for j in range(BANKS):
+                turn_add(ap, j, blocks, last=(j == BANKS - 1))
+        for j in range(BANKS - 1):
             turn_add(win2, j, range(BLK), last=True)
+        both = keep.tile([P, NB], F32, name="both")
+        for part in halves:
+            span = slice(V - NB + part.start, V - NB + part.stop)
+            nc.gpsimd.tensor_tensor(out=both[:, part], in0=win1[:, span], in1=win2[:, span], op=ALU.add)
 
         turned = keep.tile([P, V], F32, name="turned")
-        res = keep.tile([P, V], F32, name="res")
-        for j in range(BANKS):
+        res = keep.tile([P, V - NB], F32, name="res")
+        for j in (3, 0, 1, 2):
             nc.scalar.copy(out=turned[:, cols(j)], in_=bank_a[j][:])
             for b in range(BLK):
                 c0 = j * NB + b * P
@@ -232,6 +235,10 @@ def tile_attend_hvrankshares_heads_kernel(tc, hid, voc_words, voc_scales, sw, dh
         pieces = [(0, 0, NB), (1, 0, NB), (2, 0, NB), (3, 0, NB // 2), (3, NB // 2, NB)]
         for n, (j, lo, hi) in enumerate(pieces):
             span = slice(j * NB + lo, j * NB + hi)
-            nc.vector.tensor_tensor(out=res[:, span], in0=bank_t[j][:, lo:hi], in1=win1[:, span], op=ALU.add)
+            if j == BANKS - 1:
+                dst, other = turned[:, 2 * NB + lo:2 * NB + hi], both[:, lo:hi]
+            else:
+                dst, other = res[:, span], win1[:, span]
+            nc.vector.tensor_tensor(out=dst, in0=bank_t[j][:, lo:hi], in1=other, op=ALU.add)
             queue = nc.sync if n % 2 == 0 else nc.scalar
-            queue.dma_start(out=out[:, span], in_=res[:, span])
+            queue.dma_start(out=out[:, span], in_=dst)

@@ -164,28 +164,30 @@ def tile_attend_hvrankshares_heads_kernel(tc, hid, voc_words, voc_scales, sw, dh
                                            op0=op0, op1=op1, accum_out=accum)
 
         halves = (slice(0, I // 2), slice(I // 2, I))
-        gsum = keep.tile([P, 2], F32, name="gsum")
-        ssum = keep.tile([P, 7], F32, name="ssum")
+        gsum = keep.tile([P, 3], F32, name="gsum")
+        ssum = keep.tile([P, 5], F32, name="ssum")
         gn, gs2, gs1, y2, y1 = vec("gn", "slot_gn"), vec("gs2"), vec("gs1"), vec("y2"), vec("y1")
         ysum, bend, b2, b1 = vec("ysum"), vec("bend"), vec("b2"), vec("b1")
         nc.vector.tensor_copy(t1[:], ta_sb[:].indirect(list1[:]))
-        stt(gn, sq, -1.0, sw_all, ALU.add, ALU.mult)
-        stt(gs2, gn, rf[:, one(1)], px2, ALU.mult, ALU.mult, gsum[:, one(0)])
-        stt(gs1, gn, rf[:, one(0)], px, ALU.mult, ALU.mult, gsum[:, one(1)])
+        for part in halves:
+            stt(gn, sq, -1.0, sw_all, ALU.add, ALU.mult, None, part)
+        for h, part in enumerate(halves):
+            stt(gs2, gn, rf[:, one(1)], px2, ALU.mult, ALU.mult, gsum[:, one(h)], part)
+        stt(gs1, gn, rf[:, one(0)], px, ALU.mult, ALU.mult, gsum[:, one(2)])
         win2 = keep.tile([P, V], F32, name="win2", tag="slot_ta")
         nc.gpsimd.memset(win2[:], 0.0)
         win1 = keep.tile([P, V], F32, name="win1", tag="slot_gn")
         nc.gpsimd.memset(win1[:], 0.0)
-        stt(y2, t2, neg_e[:], gs2, ALU.add, ALU.mult, ssum[:, one(0)])
-        for h, part in enumerate(halves):
-            stt(y1, t1, neg_e[:], gs1, ALU.add, ALU.mult, ssum[:, one(1 + h)], part)
+        stt(y2, t2, neg_e[:], gs2, ALU.add, ALU.mult)
+        for part in halves:
+            stt(y1, t1, neg_e[:], gs1, ALU.add, ALU.mult, None, part)
         for part in halves:
             nc.vector.tensor_tensor(out=ysum[:, part], in0=y2[:, part], in1=y1[:, part], op=ALU.add)
         for part in halves:
             stt(bend, ysum, rf[:, one(2)], th, ALU.mult, ALU.mult, None, part)
         for h, part in enumerate(halves):
-            stt(b2, bend, 1.0, px2, ALU.mult, ALU.mult, ssum[:, one(3 + h)], part)
-        stt(b1, bend, -1.0, px, ALU.mult, ALU.mult, ssum[:, one(5)])
+            stt(b2, bend, 1.0, px2, ALU.mult, ALU.mult, ssum[:, one(1 + h)], part)
+        stt(b1, bend, -1.0, px, ALU.mult, ALU.mult, ssum[:, one(3)])
         nc.vector.tensor_tensor(win2[:].indirect(list2[:]), y2[:], b2[:], ALU.add)
         nc.vector.tensor_tensor(win1[:].indirect(list1[:]), y1[:], b1[:], ALU.add)
 
@@ -198,18 +200,20 @@ def tile_attend_hvrankshares_heads_kernel(tc, hid, voc_words, voc_scales, sw, dh
         for j in range(BANKS):
             turn_add(base_sb, j, range(BLK), first=True)
 
-        scrap2 = keep.tile([P, 2], F32, name="scrap2")
-        scrap2b = keep.tile([P, 2], F32, name="scrap2b")
-        scrap3 = keep.tile([P, 7], F32, name="scrap3")
+        scrap2 = keep.tile([P, 3], F32, name="scrap2")
+        scrap2b = keep.tile([P, 3], F32, name="scrap2b")
+        scrap3 = keep.tile([P, 5], F32, name="scrap3")
         beta = keep.tile([P, 1], F32, name="beta")
         stot = keep.tile([P, 1], F32, name="stot")
         alpha = keep.tile([P, BANKS], F32, name="alpha")
         nc.scalar.activation(out=scrap2[:], in_=gsum[:], func=ACT.Copy, scale=rf[:, one(3)], accum_out=beta[:])
-        nc.scalar.activation(out=scrap2b[:], in_=gsum[:], func=ACT.Copy, scale=neg_e[:], accum_out=ssum[:, one(6)])
+        nc.scalar.activation(out=scrap2b[:], in_=gsum[:], func=ACT.Copy, scale=neg_e[:], accum_out=ssum[:, one(4)])
         bxp = keep.tile([P, V], F32, name="bxp")
         for j in range(BANKS):
             nc.scalar.activation(out=bxp[:, cols(j)], in_=xp_sb[:, cols(j)], func=ACT.Copy, scale=beta[:])
             turn_add(bxp, j, range(BLK))
+        ycopy = vec("ycopy")
+        nc.scalar.activation(out=ycopy[:], in_=ysum[:], func=ACT.Copy, accum_out=ssum[:, one(0)])
         nc.scalar.activation(out=scrap3[:], in_=ssum[:], func=ACT.Copy, accum_out=stot[:])
         nc.scalar.activation(out=alpha[:], in_=neg_share[:], func=ACT.Copy, scale=stot[:])
         ap = keep.tile([P, V], F32, name="ap")
@@ -232,7 +236,7 @@ def tile_attend_hvrankshares_heads_kernel(tc, hid, voc_words, voc_scales, sw, dh
             for b in range(BLK):
                 c0 = j * NB + b * P
                 nc.tensor.transpose(bank_t[j][:, b * P:(b + 1) * P], turned[:, c0:c0 + P], ident[:])
-        pieces = [(0, 0, NB), (1, 0, NB), (2, 0, NB), (3, 0, NB // 2), (3, NB // 2, NB)]
+        pieces = [(0, 0, P), (0, P, NB), (1, 0, NB), (2, 0, NB), (3, 0, NB // 2), (3, NB // 2, NB)]
         for n, (j, lo, hi) in enumerate(pieces):
             span = slice(j * NB + lo, j * NB + hi)
             if j == BANKS - 1:

from contextlib import ExitStack

import concourse.mybir as mybir
from concourse.masks import make_identity

D, V, Q, I = 512, 2048, 128, 512
FLOPS = 2 * 2 * D * V * Q

F32 = mybir.dt.float32
BF16 = mybir.dt.bfloat16
I32 = mybir.dt.int32
U32 = mybir.dt.uint32
U16 = mybir.dt.uint16
U8 = mybir.dt.uint8
FP8X4 = mybir.dt.float8_e4m3fn_x4
FP4X4 = mybir.dt.float4_e2m1fn_x4
ALU = mybir.AluOpType
ACT = mybir.ActivationFunctionType
AX = mybir.AxisListType

P = 128
PACK = 4
NB = 512
BANKS = V // NB
BLK = NB // P
SHARP = 512.0


def tile_attend_hvrankshares_heads_kernel(tc, hid, voc_words, voc_scales, sw, dhid, base, offs, offs2, out):
    nc = tc.nc
    with ExitStack() as ctx:
        keep = ctx.enter_context(tc.tile_pool(name="keep", bufs=1))
        psum = ctx.enter_context(tc.psum_pool(name="psum", bufs=1))

        def cols(j):
            return slice(j * NB, (j + 1) * NB)

        def one(j):
            return slice(j, j + 1)

        list1 = keep.tile([P, I // 16], U16, name="list1")
        list2 = keep.tile([P, I // 16], U16, name="list2")
        vscale = keep.tile([P, V], U8, name="vscale", align_bytes=64)
        nc.vector.memset(vscale[:].bitcast(I32), 0)

        hid_raw = keep.tile([P, PACK, Q], F32, name="hid_raw", tag="stage_h")
        nc.sync.dma_start(out=hid_raw[:], in_=hid.rearrange("(p j) q -> p j q", j=PACK))
        scale_rows = voc_scales[0].bitcast(I32).rearrange("(g r) c -> r g c", r=4)
        for r in range(4):
            nc.sync.dma_start(out=vscale[r:P:32, :].bitcast(I32), in_=scale_rows[r])
        words = [keep.tile([P, V], U8, name="words%d" % h, align_bytes=64) for h in range(2)]
        dhid_raw = keep.tile([P, PACK, Q], F32, name="dhid_raw", tag="stage_d")
        nc.sync.dma_start(out=words[0][:].bitcast(I32), in_=voc_words[0][:, 0:V].bitcast(I32))
        nc.sync.dma_start(out=dhid_raw[:], in_=dhid.rearrange("(p j) q -> p j q", j=PACK))
        nc.sync.dma_start(out=words[1][:].bitcast(I32), in_=voc_words[0][:, V:2 * V].bitcast(I32))
        nc.sync.dma_start(list2[:], offs2)
        nc.sync.dma_start(list1[:], offs)

        factors = keep.tile([P, 4], F32, name="factors")
        for j, value in enumerate((SHARP / 2, -SHARP / 2, -SHARP, -1.0)):
            nc.vector.memset(factors[:, one(j)], value)
        warm = keep.tile([P, 1], F32, name="warm")
        nc.scalar.activation(out=warm[:], in_=factors[:, one(3)], func=ACT.Exp)

        ident = keep.tile([P, P], F32, name="ident")
        make_identity(nc, ident[:])

        hid_bf = keep.tile([P, Q, PACK], BF16, name="hid_bf", align_bytes=64)
        dhid_bf = keep.tile([P, Q, PACK], BF16, name="dhid_bf", align_bytes=64)
        hq = keep.tile([P, Q], U32, name="hq", align_bytes=64)
        hs = keep.tile([P, Q], U8, name="hs", align_bytes=64)
        dq = keep.tile([P, Q], U32, name="dq", align_bytes=64)
        ds = keep.tile([P, Q], U8, name="ds", align_bytes=64)
        nc.vector.tensor_copy(out=hid_bf[:], in_=hid_raw[:].rearrange("p j q -> p q j"))
        nc.vector.quantize_mx(out=hq[:].bitcast(FP8X4), scales=hs[:], in_=hid_bf[:].rearrange("p q j -> p (q j)"))
        nc.scalar.copy(out=dhid_bf[:], in_=dhid_raw[:].rearrange("p j q -> p q j"))
        nc.vector.quantize_mx(out=dq[:].bitcast(FP8X4), scales=ds[:], in_=dhid_bf[:].rearrange("p q j -> p (q j)"))

        sw_all = keep.tile([P, I], F32, name="sw_all", tag="stage_d")
        nc.sync.dma_start(out=sw_all[:], in_=sw[0].partition_broadcast(P))
        base_sb = keep.tile([P, V], F32, name="base_sb", tag="stage_h")
        nc.sync.dma_start(out=base_sb[:], in_=base)

        bank_a = [psum.tile([P, NB], F32, name="bank_a%d" % j) for j in range(BANKS)]
        bank_t = [psum.tile([P, NB], F32, name="bank_t%d" % j) for j in range(BANKS)]

        def product(bank, codes, scales, j):
            lo = (j % 2) * 2 * NB
            nc.tensor.matmul_mx(out=bank[:], lhsT=codes[:].bitcast(FP8X4), lhsT_scale=scales[:],
                                rhs=words[j // 2][:, lo:lo + 2 * NB].bitcast(FP4X4), rhs_scale=vscale[:, cols(j)],
                                start=True, stop=True)

        for j in range(BANKS):
            product(bank_a[j], hq, hs, j)
        for j in range(BANKS):
            product(bank_t[j], dq, ds, j)

        a_sb = keep.tile([P, V], F32, name="a_sb")
        ta_sb = keep.tile([P, V], F32, name="ta_sb", tag="slot_ta")
        p_sb = keep.tile([P, V], F32, name="p_sb")
        xp_sb = keep.tile([P, V], F32, name="xp_sb")
        mx = keep.tile([P, BANKS], F32, name="mx")
        neg_mx = keep.tile([P, BANKS], F32, name="neg_mx")
        zpart = keep.tile([P, BANKS], F32, name="zpart")
        xzpart = keep.tile([P, BANKS], F32, name="xzpart")
        for j in range(BANKS):
            nc.vector.tensor_scalar(out=a_sb[:, cols(j)], in0=bank_a[j][:], scalar1=1.0, scalar2=None,
                                    op0=ALU.mult, op1=ALU.max, accum_out=mx[:, one(j)])
            nc.gpsimd.tensor_scalar(out=neg_mx[:, one(j)], in0=mx[:, one(j)], scalar1=-1.0, scalar2=0.0,
                                    op0=ALU.mult, op1=ALU.add)
            nc.scalar.activation(out=p_sb[:, cols(j)], in_=a_sb[:, cols(j)], func=ACT.Exp,
                                 bias=neg_mx[:, one(j)], accum_out=zpart[:, one(j)])
        neg_m = keep.tile([P, 1], F32, name="neg_m")
        nc.vector.tensor_reduce(out=neg_m[:], in_=mx[:], axis=AX.X, op=ALU.max, negate=True)
        shift = keep.tile([P, BANKS], F32, name="shift")
        nc.scalar.activation(out=shift[:], in_=mx[:], func=ACT.Exp, bias=neg_m[:])

        def vec(name, tag=None):
            return keep.tile([P, I], F32, name=name, tag=tag or name)

        ga2, ga1, px, px2 = vec("ga2"), vec("ga1"), vec("px"), vec("px2")
        nc.vector.tensor_copy(ga2[:], a_sb[:].indirect(list2[:]))
        nc.vector.tensor_copy(ga1[:], a_sb[:].indirect(list1[:]))
        nc.scalar.copy(out=ta_sb[:, cols(0)], in_=bank_t[0][:])
        nc.scalar.activation(out=px2[:], in_=ga2[:], func=ACT.Exp, bias=neg_m[:])
        nc.scalar.copy(out=ta_sb[:, cols(1)], in_=bank_t[1][:])
        nc.scalar.activation(out=px[:], in_=ga1[:], func=ACT.Exp, bias=neg_m[:])

        zs = keep.tile([P, BANKS], F32, name="zs")
        z = keep.tile([P, 1], F32, name="z")
        rz = keep.tile([P, 1], F32, name="rz")
        rf = keep.tile([P, 4], F32, name="rf")
        neg_share = keep.tile([P, BANKS], F32, name="neg_share")
        xzs = keep.tile([P, BANKS], F32, name="xzs")
        neg_e = keep.tile([P, 1], F32, name="neg_e")
        delta, th, sq = vec("delta"), vec("th"), vec("sq")

        def xp_bank(j):
            nc.vector.scalar_tensor_tensor(out=xp_sb[:, cols(j)], in0=bank_t[j][:], scalar=shift[:, one(j)],
                                           in1=p_sb[:, cols(j)], op0=ALU.mult, op1=ALU.mult,
                                           accum_out=xzpart[:, one(j)])

        nc.vector.scalar_tensor_tensor(out=zs[:], in0=zpart[:], scalar=1.0, in1=shift[:], op0=ALU.mult, op1=ALU.mult,
                                       accum_out=z[:])
        xp_bank(3)
        nc.scalar.copy(out=ta_sb[:, cols(3)], in_=bank_t[3][:])
        nc.vector.reciprocal(rz[:], z[:])
        xp_bank(2)
        nc.scalar.copy(out=ta_sb[:, cols(2)], in_=bank_t[2][:])
        nc.scalar.activation(out=rf[:], in_=factors[:], func=ACT.Copy, scale=rz[:])
        xp_bank(1)
        nc.gpsimd.tensor_tensor(out=delta[:], in0=px2[:], in1=px[:], op=ALU.subtract)
        xp_bank(0)
        nc.scalar.activation(out=th[:], in_=delta[:], func=ACT.Tanh, scale=rf[:, one(0)])
        nc.scalar.activation(out=sq[:], in_=th[:], func=ACT.Square)
        nc.scalar.activation(out=neg_share[:], in_=shift[:], func=ACT.Copy, scale=rf[:, one(3)])

        t2, t1 = vec("t2"), vec("t1")
        nc.vector.tensor_copy(t2[:], ta_sb[:].indirect(list2[:]))
        nc.scalar.activation(out=xzs[:], in_=xzpart[:], func=ACT.Copy, scale=rf[:, one(3)], accum_out=neg_e[:])

        def stt(res, in0, scalar, in1, op0, op1, accum=None, part=slice(0, I)):
            nc.vector.scalar_tensor_tensor(out=res[:, part], in0=in0[:, part], scalar=scalar, in1=in1[:, part],
                                           op0=op0, op1=op1, accum_out=accum)

        halves = (slice(0, I // 2), slice(I // 2, I))
        gsum = keep.tile([P, 3], F32, name="gsum")
        ssum = keep.tile([P, 5], F32, name="ssum")
        gn, gs2, gs1, y2, y1 = vec("gn", "slot_gn"), vec("gs2"), vec("gs1"), vec("y2"), vec("y1")
        ysum, bend, b2, b1 = vec("ysum"), vec("bend"), vec("b2"), vec("b1")
        nc.vector.tensor_copy(t1[:], ta_sb[:].indirect(list1[:]))
        for part in halves:
            stt(gn, sq, -1.0, sw_all, ALU.add, ALU.mult, None, part)
        for h, part in enumerate(halves):
            stt(gs2, gn, rf[:, one(1)], px2, ALU.mult, ALU.mult, gsum[:, one(h)], part)
        stt(gs1, gn, rf[:, one(0)], px, ALU.mult, ALU.mult, gsum[:, one(2)])
        win2 = keep.tile([P, V], F32, name="win2", tag="slot_ta")
        nc.gpsimd.memset(win2[:], 0.0)
        win1 = keep.tile([P, V], F32, name="win1", tag="slot_gn")
        nc.gpsimd.memset(win1[:], 0.0)
        stt(y2, t2, neg_e[:], gs2, ALU.add, ALU.mult)
        for part in halves:
            stt(y1, t1, neg_e[:], gs1, ALU.add, ALU.mult, None, part)
        for part in halves:
            nc.vector.tensor_tensor(out=ysum[:, part], in0=y2[:, part], in1=y1[:, part], op=ALU.add)
        for part in halves:
            stt(bend, ysum, rf[:, one(2)], th, ALU.mult, ALU.mult, None, part)
        for h, part in enumerate(halves):
            stt(b2, bend, 1.0, px2, ALU.mult, ALU.mult, ssum[:, one(1 + h)], part)
        stt(b1, bend, -1.0, px, ALU.mult, ALU.mult, ssum[:, one(3)])
        nc.vector.tensor_tensor(win2[:].indirect(list2[:]), y2[:], b2[:], ALU.add)
        nc.vector.tensor_tensor(win1[:].indirect(list1[:]), y1[:], b1[:], ALU.add)

        def turn_add(src, j, blocks, first=False, last=False):
            for b in blocks:
                c0 = j * NB + b * P
                nc.tensor.matmul(out=bank_a[j][:, b * P:(b + 1) * P], lhsT=src[:, c0:c0 + P], rhs=ident[:],
                                 start=(first and b == 0), stop=(last and b == BLK - 1), is_transpose=True)

        for j in range(BANKS):
            turn_add(base_sb, j, range(BLK), first=True)

        scrap2 = keep.tile([P, 3], F32, name="scrap2")
        scrap2b = keep.tile([P, 3], F32, name="scrap2b")
        scrap3 = keep.tile([P, 5], F32, name="scrap3")
        beta = keep.tile([P, 1], F32, name="beta")
        stot = keep.tile([P, 1], F32, name="stot")
        alpha = keep.tile([P, BANKS], F32, name="alpha")
        nc.scalar.activation(out=scrap2[:], in_=gsum[:], func=ACT.Copy, scale=rf[:, one(3)], accum_out=beta[:])
        nc.scalar.activation(out=scrap2b[:], in_=gsum[:], func=ACT.Copy, scale=neg_e[:], accum_out=ssum[:, one(4)])
        bxp = keep.tile([P, V], F32, name="bxp")
        for j in range(BANKS):
            nc.scalar.activation(out=bxp[:, cols(j)], in_=xp_sb[:, cols(j)], func=ACT.Copy, scale=beta[:])
            turn_add(bxp, j, range(BLK))
        ycopy = vec("ycopy")
        nc.scalar.activation(out=ycopy[:], in_=ysum[:], func=ACT.Copy, accum_out=ssum[:, one(0)])
        nc.scalar.activation(out=scrap3[:], in_=ssum[:], func=ACT.Copy, accum_out=stot[:])
        nc.scalar.activation(out=alpha[:], in_=neg_share[:], func=ACT.Copy, scale=stot[:])
        ap = keep.tile([P, V], F32, name="ap")
        for blocks in (range(0, BLK - 1), range(BLK - 1, BLK)):
            for j in range(BANKS):
                span = slice(j * NB + blocks.start * P, j * NB + blocks.stop * P)
                nc.scalar.activation(out=ap[:, span], in_=p_sb[:, span], func=ACT.Copy, scale=alpha[:, one(j)])
                turn_add(ap, j, blocks, last=(j == BANKS - 1))
        for j in range(BANKS - 1):
            turn_add(win2, j, range(BLK), last=True)
        both = keep.tile([P, NB], F32, name="both")
        for part in halves:
            span = slice(V - NB + part.start, V - NB + part.stop)
            nc.gpsimd.tensor_tensor(out=both[:, part], in0=win1[:, span], in1=win2[:, span], op=ALU.add)

        turned = keep.tile([P, V], F32, name="turned")
        res = keep.tile([P, V - NB], F32, name="res")
        for j in (3, 0, 1, 2):
            nc.scalar.copy(out=turned[:, cols(j)], in_=bank_a[j][:])
            for b in range(BLK):
                c0 = j * NB + b * P
                nc.tensor.transpose(bank_t[j][:, b * P:(b + 1) * P], turned[:, c0:c0 + P], ident[:])
        pieces = [(0, 0, P), (0, P, NB), (1, 0, NB), (2, 0, NB), (3, 0, NB // 2), (3, NB // 2, NB)]
        for n, (j, lo, hi) in enumerate(pieces):
            span = slice(j * NB + lo, j * NB + hi)
            if j == BANKS - 1:
                dst, other = turned[:, 2 * NB + lo:2 * NB + hi], both[:, lo:hi]
            else:
                dst, other = res[:, span], win1[:, span]
            nc.vector.tensor_tensor(out=dst, in0=bank_t[j][:, lo:hi], in1=other, op=ALU.add)
            queue = nc.sync if n % 2 == 0 else nc.scalar
            queue.dma_start(out=out[:, span], in_=dst)
